import numpy as np
import ml_dtypes


def mxq(x, axis, fmt="e4m3"):
    dtype, down = {"e4m3": (ml_dtypes.float8_e4m3fn, 7), "e5m2": (ml_dtypes.float8_e5m2, 14)}[fmt]
    v = np.moveaxis(np.asarray(x, np.float32).astype(ml_dtypes.bfloat16).astype(np.float64), axis, -1)
    blocks = v.reshape(v.shape[:-1] + (-1, 32))
    amax = np.abs(blocks).max(-1, keepdims=True)
    byte = np.maximum(np.where(amax > 0, np.frexp(amax)[1] - 1 + 127, 0) - down, 1)
    scale = np.exp2(byte - 127.0)
    codes = (blocks / scale).astype(np.float32).astype(dtype).astype(np.float64)
    return np.moveaxis((codes * scale).reshape(v.shape), -1, axis)


WIDE = False


def mx_kscale(k):
    if not WIDE:
        return np.ones(k)
    levels = np.array([10, -10, 5, -5, 0])
    if k % 512:
        return np.exp2(np.random.permutation(np.resize(levels, k // 32))).repeat(32)
    a = np.empty((k // 512, 16))
    for p in range(k // 512):
        a[p, :8] = np.random.permutation(np.resize(levels, 8))
        for g in range(8):
            far = levels[np.abs(levels - a[p, g]) >= 10]
            a[p, g + 8] = far[np.random.randint(len(far))]
    return np.exp2(a.ravel()).repeat(32)


def f64(x):
    return np.asarray(x).astype(np.float64)


def striped(idx):
    return np.tile(idx.reshape(-1, 16).T, (8, 1)).astype(np.uint16)


def unstriped(offs):
    return offs[:16].T.reshape(-1).astype(np.int64)


E2M1 = np.array([0.0, 0.5, 1.0, 1.5, 2.0, 3.0, 4.0, 6.0, -0.0, -0.5, -1.0, -1.5, -2.0, -3.0, -4.0, -6.0])


def pack_weight(w, fmt):
    k, n = w.shape
    w = f64(np.asarray(w, np.float32).astype(ml_dtypes.bfloat16)).reshape(k // 32, 32, n)
    amax = np.abs(w).max(1)
    if fmt == "e4m3":
        byte = np.frexp(amax)[1] - 1 + 127 - 7
    else:
        mant, ex = np.frexp(amax / 6.0)
        byte = np.where(mant > 0.5, ex, ex - 1) + 127
    byte = np.clip(np.where(amax > 0, byte, 1), 1, 254)
    scaled = (w * np.exp2(127.0 - byte)[:, None, :]).reshape(k, n).astype(np.float32)
    by_word = np.ascontiguousarray(scaled.reshape(k // 512, 128, 4, n).transpose(0, 1, 3, 2))
    if fmt == "e4m3":
        words = by_word.astype(ml_dtypes.float8_e4m3fn).view(np.uint8)
    else:
        c = by_word.astype(ml_dtypes.float4_e2m1fn).view(np.uint8) & 0xF
        words = (c[..., 0::2] | (c[..., 1::2] << 4)).reshape(k // 512, 128, 2 * n)
    return np.ascontiguousarray(words), np.ascontiguousarray(byte.astype(np.uint8).reshape(k // 512, 16, n))


def unpack_weight(words, scales, fmt):
    g, _, n = scales.shape
    words = np.ascontiguousarray(words).reshape(g, 128, n, -1)
    if fmt == "e4m3":
        vals = words.view(ml_dtypes.float8_e4m3fn).astype(np.float64)
    else:
        nib = np.empty((g, 128, n, 4), np.uint8)
        nib[..., 0::2] = words & 0xF
        nib[..., 1::2] = words >> 4
        vals = E2M1[nib]
    vals = vals * np.repeat(np.exp2(scales.astype(np.float64) - 127.0), 8, axis=1)[..., None]
    return vals.transpose(0, 1, 3, 2).reshape(g * 512, n)


def gelu(v):
    return 0.5 * v * (1.0 + np.tanh(np.sqrt(2.0 / np.pi) * (v + 0.044715 * v**3)))


K, K2, H, N, T, S, T2, P = 1024, 512, 1024, 512, 2048, 512, 2048, 1024

def setup_inputs():
    n = np.random.standard_normal
    s, s2, u = mx_kscale(K)[:, None], mx_kscale(K2)[:, None], mx_kscale(H)[:, None]
    d = {}
    d["tab_words"], d["tab_scales"] = pack_weight(n((K, T)) * s, "e4m3")
    d["tab2_words"], d["tab2_scales"] = pack_weight(n((K2, T)) * s2, "e4m3")
    d["offs"] = striped(np.random.permutation(T)[:S])
    d["offs2"] = striped(np.random.permutation(T)[:S])
    perm = np.random.permutation(T2)
    d["offs3"] = striped(perm[:S])
    d["offs4"] = striped(perm[S:2 * S])
    d["offs5"] = striped(np.random.permutation(T2)[:P])
    d["w1"] = (n((K, H)) / K**0.5 / s).astype(np.float32)
    d["wd_words"], d["wd_scales"] = pack_weight((0.8 * np.eye(K, H) + 0.6 * n((K, H)) / K**0.5) / s, "e4m3")
    d["w4_words"], d["w4_scales"] = pack_weight(3.0 * n((K2, H)) / K2**0.5 / s2, "e2m1")
    d["wg1"] = np.exp(0.3 * n((128, S))).astype(np.float32)
    d["wg2"] = np.exp(0.3 * n((128, S))).astype(np.float32)
    d["page0"] = (1.2 * n((H, T2))).astype(np.float32)
    d["go"] = (np.exp(0.3 * n(H)) * u[:, 0]).astype(np.float32)
    d["w3"] = (1.5 * n((H, N)) / H**0.5 / u).astype(np.float32)
    d["expect"] = (0.8 * n((N, P))).astype(np.float32)
    return d

def reference(tab_words, tab_scales, tab2_words, tab2_scales, offs, offs2, offs3, offs4, offs5, w1, wd_words, wd_scales, w4_words, w4_scales, wg1, wg2, page0, go, w3, expect):
    v = unpack_weight(tab_words, tab_scales, "e4m3")[:, unstriped(offs)]
    v2 = unpack_weight(tab2_words, tab2_scales, "e4m3")[:, unstriped(offs2)]
    p1 = mxq(f64(w1), 0, "e4m3").T @ v
    pd = unpack_weight(wd_words, wd_scales, "e4m3").T @ v
    h1 = np.maximum(p1, pd)
    t2 = unpack_weight(w4_words, w4_scales, "e2m1").T @ v2
    h2 = np.log(1.0 + np.abs(t2))
    page = f64(page0).copy()
    page[:, unstriped(offs3)] = np.tile(f64(wg1), (H // 128, 1)) * h1
    page[:, unstriped(offs4)] = np.tile(f64(wg2), (H // 128, 1)) * h2
    z = np.tanh(page[:, unstriped(offs5)]) * f64(go)[:, None]
    y = mxq(f64(w3), 0, "e4m3").T @ mxq(z, 0, "e4m3")
    return np.square(y - f64(expect))

@@ -1,0 +1,378 @@
+from contextlib import ExitStack
+
+import concourse.mybir as mybir
+
+K, K2, H, N, T, S, T2, J = 1024, 512, 1024, 512, 2048, 512, 2048, 1024
+FLOPS = 2 * (2 * K * H * S + K2 * H * S + H * N * J)
+
+F32 = mybir.dt.float32
+BF16 = mybir.dt.bfloat16
+I32 = mybir.dt.int32
+U32 = mybir.dt.uint32
+U16 = mybir.dt.uint16
+U8 = mybir.dt.uint8
+FP8X4 = mybir.dt.float8_e4m3fn_x4
+FP4X4 = mybir.dt.float4_e2m1fn_x4
+ACT = mybir.ActivationFunctionType
+ALU = mybir.AluOpType
+
+P = 128
+PACK = 4
+KP = P * PACK
+NB = 512
+TILES = H // P
+HALVES = J // NB
+LAST = 64
+
+
+def tile_list_fog_net_yield_kernel(
+    tc, tab_words, tab_scales, tab2_words, tab2_scales, offs, offs2, offs3, offs4, offs5,
+    w1, wd_words, wd_scales, w4_words, w4_scales, wg1, wg2, page0, go, w3, expect, out,
+):
+    nc = tc.nc
+    with ExitStack() as ctx:
+        sb = ctx.enter_context(tc.tile_pool(name="sb", bufs=1))
+        ps = ctx.enter_context(tc.psum_pool(name="ps", bufs=4))
+
+        def new(name, shape, dtype, tag=None, bufs=1):
+            return sb.tile(shape, dtype, name=name, tag=tag or name, bufs=bufs, align_bytes=64)
+
+        def load_list(name, src):
+            dst = new(name, list(src.shape), U16)
+            nc.sync.dma_start(dst[:], src)
+            return dst
+
+        def zeroed_plane(engine, name, width):
+            plane = new(name, [P, width], U8)
+            engine.memset(plane[:].bitcast(I32), 0)
+            return plane
+
+        def load_scale_rows(plane, src, quadrants):
+            passes = src.shape[0]
+            for q in quadrants:
+                nc.sync.dma_start(
+                    plane[32 * q : 32 * q + 4 * passes, :].bitcast(I32),
+                    src[:, 4 * q : 4 * q + 4, :].bitcast(I32),
+                )
+
+        def load_words(name, src):
+            dst = new(name, [P, T], I32)
+            nc.sync.dma_start(dst[:], src.rearrange("p t i -> p (t i)").bitcast(I32))
+            return dst
+
+        def load_dealt(name, src, first, count, queues):
+            dst = new(name, [P, count * S], F32)
+            rows = src.rearrange("(m t) j -> m (t j)", t=PACK)[:, S * first : S * (first + count)]
+            for q in range(4):
+                queues[q].dma_start(dst[32 * q : 32 * q + 32, :], rows)
+            return [dst[:, S * t : S * (t + 1)] for t in range(count)]
+
+        def load_page(i):
+            b, t = divmod(i, PACK)
+            dst = new("page%d" % i, [P, T2], F32)
+            nc.sync.dma_start(dst[:], page0[KP * b : KP * (b + 1), :].rearrange("(p t) c -> p t c", t=PACK)[:, t, :])
+            return dst
+
+        def load_rows(name, src):
+            dst = new(name, [P, PACK, NB], F32, tag="stage", bufs=3)
+            nc.sync.dma_start(dst[:], src.rearrange("(p i) c -> p i c", i=PACK))
+            return dst
+
+        def load_w1(b, a):
+            return load_rows("w1raw%d%d" % (b, a), w1[KP * a : KP * (a + 1), KP * b : KP * (b + 1)])
+
+        def load_wd(b):
+            dst = new("wdraw%d" % b, [P, 2, KP], I32, tag="ring4k", bufs=3)
+            src = wd_words.rearrange("a p c i -> p a (c i)")[:, :, PACK * KP * b : PACK * KP * (b + 1)]
+            nc.sync.dma_start(dst[:], src.bitcast(I32))
+            return dst
+
+        def gather_words(name, table, lst):
+            dst = new(name, [P, S], U32)
+            nc.vector.tensor_copy(dst[:], table[:].bitcast(U32).indirect(lst[:]))
+            return dst
+
+        def gather_scales(name, plane, lst):
+            dst = new(name, [P, S], U8)
+            nc.vector.tensor_copy(dst[:], plane[:].indirect(lst[:]))
+            return dst
+
+        def deal_scales(name, plane, b):
+            dst = new(name, [P, KP], U8)
+            nc.vector.tensor_copy(
+                dst[:].rearrange("p (t m) -> p m t", t=PACK),
+                plane[:, KP * b : KP * (b + 1)].rearrange("p (m t) -> p m t", t=PACK),
+            )
+            return dst
+
+        def deal_w4(b, raw):
+            dst = new("w4_%d" % b, [P, 2 * KP], U8)
+            nc.vector.tensor_copy(
+                dst[:].rearrange("p (t m e) -> p m t e", t=PACK, e=2),
+                raw[:, 2 * KP * b : 2 * KP * (b + 1)].rearrange("p (m t e) -> p m t e", t=PACK, e=2),
+            )
+            return dst
+
+        def deal_wd(b, raw):
+            dst = new("wd%d" % b, [P, 2 * KP], I32)
+            nc.vector.tensor_copy(
+                dst[:].rearrange("p (a t m) -> p a m t", a=2, t=PACK),
+                raw[:].rearrange("p a (m t) -> p a m t", t=PACK),
+            )
+            return dst
+
+        def quantize(name, grouped):
+            codes = new(name + "c", [P, NB], U32)
+            scales = new(name + "s", [P, NB], U8)
+            nc.vector.quantize_mx(out=codes[:].bitcast(FP8X4), scales=scales[:], in_=grouped[:])
+            return codes, scales
+
+        def round_w1(name, raw):
+            grouped = new(name, [P, PACK * NB], BF16, tag="ring4k", bufs=3)
+            nc.scalar.copy(
+                grouped[:].rearrange("p (t m i) -> p m i t", t=PACK, i=PACK),
+                raw[:].rearrange("p i (m t) -> p m i t", t=PACK),
+            )
+            return grouped
+
+        def round_w3(name, raw):
+            grouped = new(name, [P, PACK * NB], BF16, tag="ring4k", bufs=3)
+            nc.scalar.copy(
+                grouped[:].rearrange("p (c e i) -> p c i e", e=PACK, i=PACK),
+                raw[:].rearrange("p i (c e) -> p c i e", e=PACK),
+            )
+            return grouped
+
+        tab2_plane = zeroed_plane(nc.gpsimd, "tab2_plane", T)
+        w4_plane = zeroed_plane(nc.gpsimd, "w4_plane", H)
+        one = new("one", [P, 8], F32)
+        nc.vector.memset(one[:], 1.0)
+        warm = new("warm", [P, 8], F32)
+        nc.scalar.activation(warm[:], one[:], ACT.Ln)
+
+        tab_plane = zeroed_plane(nc.vector, "tab_plane", T)
+        wd_plane = zeroed_plane(nc.vector, "wd_plane", H)
+
+        idx2 = load_list("idx2", offs2)
+        w4_raw = new("w4_raw", [P, 2 * H], U8)
+        nc.sync.dma_start(w4_raw[:].bitcast(I32), w4_words[0].bitcast(I32))
+        load_scale_rows(tab2_plane, tab2_scales, range(4))
+        tab2 = load_words("tab2", tab2_words[0])
+        load_scale_rows(w4_plane, w4_scales, range(4))
+        order = [PACK * b + t for t in range(PACK) for b in range(2)]
+        pages = {order[0]: load_page(order[0])}
+        idx4 = load_list("idx4", offs4)
+        g2 = load_dealt("g2a", wg2, 0, 1, [nc.sync, nc.sync, nc.gpsimd, nc.gpsimd])
+        pages[order[1]] = load_page(order[1])
+        g2.extend(load_dealt("g2b", wg2, 1, PACK - 1, [nc.sync] * 4))
+        pages[order[2]] = load_page(order[2])
+        pages[order[3]] = load_page(order[3])
+        load_scale_rows(tab_plane, tab_scales, (0, 1))
+        w1_raw = {(0, 0): load_w1(0, 0)}
+        load_scale_rows(tab_plane, tab_scales, (2, 3))
+        pages[order[4]] = load_page(order[4])
+        load_scale_rows(wd_plane, wd_scales, (0, 1))
+        pages[order[5]] = load_page(order[5])
+        load_scale_rows(wd_plane, wd_scales, (2, 3))
+        w1_raw[(0, 1)] = load_w1(0, 1)
+        idx = load_list("idx", offs)
+        idx3 = load_list("idx3", offs3)
+        pages[order[6]] = load_page(order[6])
+        tab = [load_words("tab0", tab_words[0])]
+        idx5 = load_list("idx5", offs5)
+        gain = new("gain", [P, 2, PACK], F32)
+        nc.sync.dma_start(gain[:], go.rearrange("(b p t) -> p b t", b=2, t=PACK))
+        tab.append(load_words("tab1", tab_words[1]))
+        wd_raw = [load_wd(0)]
+        pages[order[7]] = load_page(order[7])
+
+        w4 = [deal_w4(0, w4_raw)]
+        v2_scales = gather_scales("v2_scales", tab2_plane, idx2)
+        v2 = gather_words("v2", tab2, idx2)
+        w4_sc = [deal_scales("w4_sc0", w4_plane, 0)]
+        w4.append(deal_w4(1, w4_raw))
+        w4_sc.append(deal_scales("w4_sc1", w4_plane, 1))
+        h2 = {}
+        for i in order:
+            b, t = divmod(i, PACK)
+            bank = ps.tile([P, S], F32, name="t2_%d" % i, tag="first")
+            nc.tensor.matmul_mx(
+                out=bank[:],
+                lhsT=w4[b][:, 2 * P * t : 2 * P * (t + 1)].bitcast(FP4X4),
+                lhsT_scale=w4_sc[b][:, P * t : P * (t + 1)],
+                rhs=v2[:].bitcast(FP8X4),
+                rhs_scale=v2_scales[:],
+                start=True,
+                stop=True,
+            )
+            if i == TILES - 1:
+                h = new("h2_%d" % i, [P, S], F32, tag="hold_a")
+            else:
+                h = new("h2_%d" % i, [P, S], F32, tag="h2", bufs=TILES - 1)
+            for lo in (0, S // 2):
+                nc.scalar.activation(h[:, lo : lo + S // 2], bank[:, lo : lo + S // 2], ACT.Abs)
+            for lo in (0, S // 2):
+                nc.scalar.activation(h[:, lo : lo + S // 2], h[:, lo : lo + S // 2], ACT.Ln, bias=1.0)
+            h2[i] = h
+
+        def put(i, lst, h, weights):
+            nc.vector.tensor_tensor(pages[i][:].indirect(lst[:]), h[:], weights[i % PACK], ALU.mult)
+
+        w1q = {}
+        for step in range(TILES - 1):
+            i = order[step]
+            put(i, idx4, h2[i], g2)
+            if step in (4, 6):
+                a = (step - 4) // 2
+                w1q[(0, a)] = quantize("w1q0%d" % a, round_w1("w1b0%d" % a, w1_raw[(0, a)]))
+        v = [gather_words("v%d" % a, tab[a], idx) for a in range(2)]
+        v_scales = gather_scales("v_scales", tab_plane, idx)
+        wd_sc = [deal_scales("wd_sc0", wd_plane, 0)]
+        wd = [deal_wd(0, wd_raw[0])]
+        put(TILES - 1, idx4, h2[TILES - 1], g2)
+
+        w1_raw[(1, 0)] = load_w1(1, 0)
+        g1 = load_dealt("g1", wg1, 0, PACK, [nc.sync] * 4)
+        w1_raw[(1, 1)] = load_w1(1, 1)
+        wd_raw.append(load_wd(1))
+
+        def droplet_sums(i):
+            b, t = divmod(i, PACK)
+            cols = slice(P * t, P * (t + 1))
+            p1 = ps.tile([P, S], F32, name="p1_%d" % i, tag="first")
+            for a in range(2):
+                codes, scales = w1q[(b, a)]
+                nc.tensor.matmul_mx(
+                    out=p1[:], lhsT=codes[:, cols].bitcast(FP8X4), lhsT_scale=scales[:, cols],
+                    rhs=v[a][:].bitcast(FP8X4), rhs_scale=v_scales[4 * a : P, :],
+                    start=(a == 0), stop=(a == 1),
+                )
+            pd = ps.tile([P, S], F32, name="pd_%d" % i, tag="first")
+            for a in range(2):
+                nc.tensor.matmul_mx(
+                    out=pd[:],
+                    lhsT=wd[b][:, KP * a + P * t : KP * a + P * (t + 1)].bitcast(FP8X4),
+                    lhsT_scale=wd_sc[b][4 * a : P, cols],
+                    rhs=v[a][:].bitcast(FP8X4), rhs_scale=v_scales[4 * a : P, :],
+                    start=(a == 0), stop=(a == 1),
+                )
+            pd_sb = new("pd_sb%d" % i, [P, S], F32, tag="pd_sb", bufs=3)
+            nc.scalar.copy(pd_sb[:], pd[:])
+            return p1, pd_sb
+
+        def maximum(i, sums):
+            if i == 0:
+                h = new("h1_%d" % i, [P, S], F32, tag="hold_a")
+            elif i == 5:
+                h = new("h1_%d" % i, [P, S], F32, tag="hold_b")
+            else:
+                h = new("h1_%d" % i, [P, S], F32, tag="h1", bufs=2)
+            nc.vector.tensor_tensor(h[:], sums[0][:], sums[1][:], ALU.max)
+            return h
+
+        sums = {i: droplet_sums(i) for i in range(2)}
+        for a in range(2):
+            w1q[(1, a)] = quantize("w1q1%d" % a, round_w1("w1b1%d" % a, w1_raw[(1, a)]))
+        wd.append(deal_wd(1, wd_raw[1]))
+        wd_sc.append(deal_scales("wd_sc1", wd_plane, 1))
+        w3_raw = [load_rows("w3raw%d" % b, w3[KP * b : KP * (b + 1), :]) for b in range(2)]
+        h1 = {0: maximum(0, sums[0])}
+        sums[2] = droplet_sums(2)
+
+        z_codes, z_scales, w3q = [], [], []
+        z_rows = {}
+        z = {}
+
+        def weave(engine_copy, u, first, count):
+            engine_copy(
+                z[u][:].rearrange("p (c e t) -> p c t e", e=PACK, t=PACK)[:, :, first : first + count, :],
+                z_rows[u][:, first : first + count, :].rearrange("p t (c e) -> p c t e", e=PACK),
+            )
+
+        def quantize_z(b, u):
+            cols = slice(NB * u, NB * (u + 1))
+            nc.vector.quantize_mx(out=z_codes[b][:, cols].bitcast(FP8X4), scales=z_scales[b][:, cols], in_=z[u][:])
+
+        scores = {}
+
+        def yield_pass(u, n, b):
+            cols = slice(NB * u, NB * (u + 1))
+            rows = slice(P * n, P * (n + 1))
+            if b == 0:
+                scores[(u, n)] = ps.tile([P, NB], F32, name="y%d%d" % (u, n), tag="second" if u == 0 else "first")
+            codes, scales = w3q[b]
+            nc.tensor.matmul_mx(
+                out=scores[(u, n)][:], lhsT=codes[:, rows].bitcast(FP8X4), lhsT_scale=scales[:, rows],
+                rhs=z_codes[b][:, cols].bitcast(FP8X4), rhs_scale=z_scales[b][:, cols],
+                start=(b == 0), stop=(b == 1),
+            )
+
+        for i in range(TILES):
+            b, t = divmod(i, PACK)
+            put(i, idx3, h1[i], g1)
+            if i + 1 < TILES:
+                h1[i + 1] = maximum(i + 1, sums[i + 1])
+            if i == 5:
+                z_codes.append(new("zc0", [P, J], U32, tag="hold_b"))
+                z_scales.append(new("zs0", [P, J], U8, tag="w4_0"))
+                for u in range(HALVES):
+                    quantize_z(0, u)
+            if i >= TILES - 2:
+                for n in range(N // P):
+                    yield_pass(i - (TILES - 2), n, 0)
+            if t == 0:
+                z_rows[0] = new("z_rows%d0" % b, [P, PACK, NB], BF16, tag="g2b")
+                z_rows[1] = new("z_rows%d1" % b, [P, PACK, NB], BF16, tag="z_rows")
+            picked = new("picked%d" % i, [P, J], F32, tag="picked", bufs=2)
+            pieces = HALVES if i == TILES - 1 else 1
+            width = J // pieces
+            for u in range(pieces):
+                cols = slice(width * u, width * (u + 1))
+                lst = idx5[:, width // 16 * u : width // 16 * (u + 1)]
+                nc.vector.tensor_copy(picked[:, cols], pages[i][:].indirect(lst))
+            factor = gain[:, b, t : t + 1]
+            if i == TILES - 1:
+                for u in range(HALVES):
+                    cols = slice(NB * u, NB * (u + 1))
+                    nc.scalar.activation(picked[:, cols], picked[:, cols], ACT.Tanh)
+                    nc.scalar.activation(z_rows[u][:, t, :], picked[:, cols], ACT.Copy, scale=factor)
+                for u in range(HALVES):
+                    weave(nc.vector.tensor_copy, u, 2, 2)
+            else:
+                for u in range(HALVES):
+                    cols = slice(NB * u, NB * (u + 1))
+                    nc.scalar.activation(picked[:, cols], picked[:, cols], ACT.Tanh)
+                for lo, hi in ((0, NB), (NB, J - LAST), (J - LAST, J)):
+                    if hi == J and i + 3 < TILES:
+                        sums[i + 3] = droplet_sums(i + 3)
+                    u = lo // NB
+                    nc.scalar.activation(
+                        z_rows[u][:, t, lo - NB * u : hi - NB * u], picked[:, lo:hi], ACT.Copy, scale=factor
+                    )
+            if i in (3, 5):
+                for u in range(HALVES):
+                    z[u] = new("z%d%d" % (b, u), [P, PACK * NB], BF16, tag="z%d" % u)
+                    weave(nc.scalar.copy, u, 0, PACK if b == 0 else 2)
+            if i in (0, 1):
+                w3q.append(quantize("w3q%d" % i, round_w3("w3b%d" % i, w3_raw[i])))
+
+        want = []
+        for u in range(2):
+            dst = new("want%d" % u, [P, 2, J], F32, tag="stage", bufs=3)
+            nc.sync.dma_start(dst[:], expect[2 * P * u : 2 * P * (u + 1), :].rearrange("(a p) j -> p a j", p=P))
+            want.append(dst)
+
+        z_codes.append(new("zc1", [P, J], U32))
+        z_scales.append(new("zs1", [P, J], U8, tag="w4_1"))
+        for u in range(HALVES):
+            quantize_z(1, u)
+        for u in range(HALVES):
+            cols = slice(NB * u, NB * (u + 1))
+            for n in range(N // P):
+                rows = slice(P * n, P * (n + 1))
+                yield_pass(u, n, 1)
+                y = scores[(u, n)]
+                diff = new("diff%d%d" % (u, n), [P, NB], F32, tag="h2", bufs=TILES - 1)
+                nc.vector.tensor_tensor(diff[:], y[:], want[n // 2][:, n % 2, cols], ALU.subtract)
+                nc.scalar.activation(diff[:], diff[:], ACT.Square)
+                nc.sync.dma_start(out[rows, cols], diff[:])

@@ -1,6 +1,7 @@
 from contextlib import ExitStack
 
 import concourse.mybir as mybir
+from concourse.masks import make_identity
 
 K, K2, H, N, T, S, T2, J = 1024, 512, 1024, 512, 2048, 512, 2048, 1024
 FLOPS = 2 * (2 * K * H * S + K2 * H * S + H * N * J)
@@ -42,15 +43,15 @@ def tile_list_fog_net_yield_kernel(
             nc.sync.dma_start(dst[:], src)
             return dst
 
-        def zeroed_plane(engine, name, width):
-            plane = new(name, [P, width], U8)
-            engine.memset(plane[:].bitcast(I32), 0)
+        def zeroed_plane(name, width, tag=None):
+            plane = new(name, [P, width], U8, tag=tag)
+            nc.gpsimd.memset(plane[:].bitcast(I32), 0)
             return plane
 
-        def load_scale_rows(plane, src, quadrants):
+        def load_scale_rows(queue, plane, src):
             passes = src.shape[0]
-            for q in quadrants:
-                nc.sync.dma_start(
+            for q in range(4):
+                queue.dma_start(
                     plane[32 * q : 32 * q + 4 * passes, :].bitcast(I32),
                     src[:, 4 * q : 4 * q + 4, :].bitcast(I32),
                 )
@@ -60,12 +61,26 @@ def tile_list_fog_net_yield_kernel(
             nc.sync.dma_start(dst[:], src.rearrange("p t i -> p (t i)").bitcast(I32))
             return dst
 
-        def load_dealt(name, src, first, count, queues):
-            dst = new(name, [P, count * S], F32)
-            rows = src.rearrange("(m t) j -> m (t j)", t=PACK)[:, S * first : S * (first + count)]
-            for q in range(4):
-                queues[q].dma_start(dst[32 * q : 32 * q + 32, :], rows)
-            return [dst[:, S * t : S * (t + 1)] for t in range(count)]
+        def load_weights(name, src):
+            dst = new(name, [P, S], F32, tag="h1", bufs=2)
+            nc.sync.dma_start(dst[:], src)
+            return dst
+
+        def turn(name, src):
+            bank = ps.tile([P, S], F32, name=name, tag="second")
+            for c in range(S // P):
+                nc.tensor.transpose(bank[:, P * c : P * (c + 1)], src[:, P * c : P * (c + 1)], ident[:])
+            return bank
+
+        def deal_weights(name, turned, t):
+            spread = new(name + "s", [P, S], F32, tag="pd_sb", bufs=3)
+            nc.scalar.copy(
+                spread[:].rearrange("p (c q m) -> p c q m", q=4, m=32),
+                turned[:].rearrange("p (c m t) -> p c t m", m=32, t=PACK)[:, :, t : t + 1, :].to_broadcast([P, S // P, 4, 32]),
+            )
+            dst = new(name, [P, S], F32)
+            nc.scalar.copy(dst[:], turn(name + "t", spread)[:])
+            return dst
 
         def load_page(i):
             b, t = divmod(i, PACK)
@@ -97,27 +112,27 @@ def tile_list_fog_net_yield_kernel(
             nc.vector.tensor_copy(dst[:], plane[:].indirect(lst[:]))
             return dst
 
-        def deal_scales(name, plane, b):
-            dst = new(name, [P, KP], U8)
+        def deal_scales(name, plane, b, tag=None):
+            dst = new(name, [P, KP], U8, tag=tag)
             nc.vector.tensor_copy(
-                dst[:].rearrange("p (t m) -> p m t", t=PACK),
-                plane[:, KP * b : KP * (b + 1)].rearrange("p (m t) -> p m t", t=PACK),
+                dst[:].rearrange("p (t c e) -> p c t e", t=PACK, e=16),
+                plane[:, KP * b : KP * (b + 1)].rearrange("p (c e t) -> p c t e", t=PACK, e=16),
             )
             return dst
 
         def deal_w4(b, raw):
             dst = new("w4_%d" % b, [P, 2 * KP], U8)
             nc.vector.tensor_copy(
-                dst[:].rearrange("p (t m e) -> p m t e", t=PACK, e=2),
-                raw[:, 2 * KP * b : 2 * KP * (b + 1)].rearrange("p (m t e) -> p m t e", t=PACK, e=2),
+                dst[:].bitcast(U16).rearrange("p (t c e) -> p c t e", t=PACK, e=8),
+                raw[:, 2 * KP * b : 2 * KP * (b + 1)].bitcast(U16).rearrange("p (c e t) -> p c t e", t=PACK, e=8),
             )
             return dst
 
         def deal_wd(b, raw):
             dst = new("wd%d" % b, [P, 2 * KP], I32)
             nc.vector.tensor_copy(
-                dst[:].rearrange("p (a t m) -> p a m t", a=2, t=PACK),
-                raw[:].rearrange("p a (m t) -> p a m t", t=PACK),
+                dst[:].rearrange("p (a t c e) -> p a c t e", a=2, t=PACK, e=4),
+                raw[:].rearrange("p a (c e t) -> p a c t e", t=PACK, e=4),
             )
             return dst
 
@@ -143,48 +158,41 @@ def tile_list_fog_net_yield_kernel(
             )
             return grouped
 
-        tab2_plane = zeroed_plane(nc.gpsimd, "tab2_plane", T)
-        w4_plane = zeroed_plane(nc.gpsimd, "w4_plane", H)
+        tab2_plane = zeroed_plane("tab2_plane", T)
+        w4_plane = zeroed_plane("w4_plane", H)
+        ident = new("ident", [P, P], F32)
+        make_identity(nc, ident[:])
         one = new("one", [P, 8], F32)
         nc.vector.memset(one[:], 1.0)
         warm = new("warm", [P, 8], F32)
         nc.scalar.activation(warm[:], one[:], ACT.Ln)
 
-        tab_plane = zeroed_plane(nc.vector, "tab_plane", T)
-        wd_plane = zeroed_plane(nc.vector, "wd_plane", H)
-
         idx2 = load_list("idx2", offs2)
+        wg2_rows = load_weights("wg2_rows", wg2)
         w4_raw = new("w4_raw", [P, 2 * H], U8)
         nc.sync.dma_start(w4_raw[:].bitcast(I32), w4_words[0].bitcast(I32))
-        load_scale_rows(tab2_plane, tab2_scales, range(4))
+        load_scale_rows(nc.sync, tab2_plane, tab2_scales)
         tab2 = load_words("tab2", tab2_words[0])
-        load_scale_rows(w4_plane, w4_scales, range(4))
+        load_scale_rows(nc.sync, w4_plane, w4_scales)
         order = [PACK * b + t for t in range(PACK) for b in range(2)]
         pages = {order[0]: load_page(order[0])}
         idx4 = load_list("idx4", offs4)
-        g2 = load_dealt("g2a", wg2, 0, 1, [nc.sync, nc.sync, nc.gpsimd, nc.gpsimd])
-        pages[order[1]] = load_page(order[1])
-        g2.extend(load_dealt("g2b", wg2, 1, PACK - 1, [nc.sync] * 4))
-        pages[order[2]] = load_page(order[2])
-        pages[order[3]] = load_page(order[3])
-        load_scale_rows(tab_plane, tab_scales, (0, 1))
+        for step in (1, 2, 3):
+            pages[order[step]] = load_page(order[step])
         w1_raw = {(0, 0): load_w1(0, 0)}
-        load_scale_rows(tab_plane, tab_scales, (2, 3))
         pages[order[4]] = load_page(order[4])
-        load_scale_rows(wd_plane, wd_scales, (0, 1))
+        wg1_rows = load_weights("wg1_rows", wg1)
         pages[order[5]] = load_page(order[5])
-        load_scale_rows(wd_plane, wd_scales, (2, 3))
         w1_raw[(0, 1)] = load_w1(0, 1)
-        idx = load_list("idx", offs)
-        idx3 = load_list("idx3", offs3)
         pages[order[6]] = load_page(order[6])
-        tab = [load_words("tab0", tab_words[0])]
+        idx = load_list("idx", offs)
+        tab = [load_words("tab%d" % a, tab_words[a]) for a in range(2)]
+        idx3 = load_list("idx3", offs3)
+        wd_raw = [load_wd(0)]
+        pages[order[7]] = load_page(order[7])
         idx5 = load_list("idx5", offs5)
         gain = new("gain", [P, 2, PACK], F32)
         nc.sync.dma_start(gain[:], go.rearrange("(b p t) -> p b t", b=2, t=PACK))
-        tab.append(load_words("tab1", tab_words[1]))
-        wd_raw = [load_wd(0)]
-        pages[order[7]] = load_page(order[7])
 
         w4 = [deal_w4(0, w4_raw)]
         v2_scales = gather_scales("v2_scales", tab2_plane, idx2)
@@ -192,9 +200,17 @@ def tile_list_fog_net_yield_kernel(
         w4_sc = [deal_scales("w4_sc0", w4_plane, 0)]
         w4.append(deal_w4(1, w4_raw))
         w4_sc.append(deal_scales("w4_sc1", w4_plane, 1))
+        tab_plane = zeroed_plane("tab_plane", T, tag="w4_raw")
+        load_scale_rows(nc.gpsimd, tab_plane, tab_scales)
+        wd_plane = zeroed_plane("wd_plane", H, tag="w4_plane")
+        load_scale_rows(nc.gpsimd, wd_plane, wd_scales)
         h2 = {}
+        g2 = []
+        wg2_turned = turn("wg2_turned", wg2_rows)
         for i in order:
             b, t = divmod(i, PACK)
+            if b == 0:
+                g2.append(deal_weights("g2_%d" % t, wg2_turned, t))
             bank = ps.tile([P, S], F32, name="t2_%d" % i, tag="first")
             nc.tensor.matmul_mx(
                 out=bank[:],
@@ -216,7 +232,7 @@ def tile_list_fog_net_yield_kernel(
             h2[i] = h
 
         def put(i, lst, h, weights):
-            nc.vector.tensor_tensor(pages[i][:].indirect(lst[:]), h[:], weights[i % PACK], ALU.mult)
+            nc.vector.tensor_tensor(pages[i][:].indirect(lst[:]), h[:], weights[i % PACK][:], ALU.mult)
 
         w1q = {}
         for step in range(TILES - 1):
@@ -225,14 +241,15 @@ def tile_list_fog_net_yield_kernel(
             if step in (4, 6):
                 a = (step - 4) // 2
                 w1q[(0, a)] = quantize("w1q0%d" % a, round_w1("w1b0%d" % a, w1_raw[(0, a)]))
+        wg1_turned = turn("wg1_turned", wg1_rows)
+        g1 = [deal_weights("g1_%d" % t, wg1_turned, t) for t in range(PACK)]
         v = [gather_words("v%d" % a, tab[a], idx) for a in range(2)]
         v_scales = gather_scales("v_scales", tab_plane, idx)
-        wd_sc = [deal_scales("wd_sc0", wd_plane, 0)]
+        wd_sc = [deal_scales("wd_sc0", wd_plane, 0, tag="g2_2")]
         wd = [deal_wd(0, wd_raw[0])]
         put(TILES - 1, idx4, h2[TILES - 1], g2)
 
         w1_raw[(1, 0)] = load_w1(1, 0)
-        g1 = load_dealt("g1", wg1, 0, PACK, [nc.sync] * 4)
         w1_raw[(1, 1)] = load_w1(1, 1)
         wd_raw.append(load_wd(1))
 
@@ -274,7 +291,7 @@ def tile_list_fog_net_yield_kernel(
         for a in range(2):
             w1q[(1, a)] = quantize("w1q1%d" % a, round_w1("w1b1%d" % a, w1_raw[(1, a)]))
         wd.append(deal_wd(1, wd_raw[1]))
-        wd_sc.append(deal_scales("wd_sc1", wd_plane, 1))
+        wd_sc.append(deal_scales("wd_sc1", wd_plane, 1, tag="g2_3"))
         w3_raw = [load_rows("w3raw%d" % b, w3[KP * b : KP * (b + 1), :]) for b in range(2)]
         h1 = {0: maximum(0, sums[0])}
         sums[2] = droplet_sums(2)
@@ -321,8 +338,8 @@ def tile_list_fog_net_yield_kernel(
                 for n in range(N // P):
                     yield_pass(i - (TILES - 2), n, 0)
             if t == 0:
-                z_rows[0] = new("z_rows%d0" % b, [P, PACK, NB], BF16, tag="g2b")
-                z_rows[1] = new("z_rows%d1" % b, [P, PACK, NB], BF16, tag="z_rows")
+                z_rows[0] = new("z_rows%d0" % b, [P, PACK, NB], BF16, tag="g2_0")
+                z_rows[1] = new("z_rows%d1" % b, [P, PACK, NB], BF16, tag="g2_1")
             picked = new("picked%d" % i, [P, J], F32, tag="picked", bufs=2)
             pieces = HALVES if i == TILES - 1 else 1
             width = J // pieces

@@ -162,6 +162,8 @@ def tile_list_fog_net_yield_kernel(
         w4_plane = zeroed_plane("w4_plane", H)
         ident = new("ident", [P, P], F32)
         make_identity(nc, ident[:])
+        tab_plane = zeroed_plane("tab_plane", T)
+        wd_plane = zeroed_plane("wd_plane", H)
         one = new("one", [P, 8], F32)
         nc.vector.memset(one[:], 1.0)
         warm = new("warm", [P, 8], F32)
@@ -179,8 +181,10 @@ def tile_list_fog_net_yield_kernel(
         idx4 = load_list("idx4", offs4)
         for step in (1, 2, 3):
             pages[order[step]] = load_page(order[step])
+        load_scale_rows(nc.sync, tab_plane, tab_scales)
         w1_raw = {(0, 0): load_w1(0, 0)}
         pages[order[4]] = load_page(order[4])
+        load_scale_rows(nc.sync, wd_plane, wd_scales)
         wg1_rows = load_weights("wg1_rows", wg1)
         pages[order[5]] = load_page(order[5])
         w1_raw[(0, 1)] = load_w1(0, 1)
@@ -200,10 +204,6 @@ def tile_list_fog_net_yield_kernel(
         w4_sc = [deal_scales("w4_sc0", w4_plane, 0)]
         w4.append(deal_w4(1, w4_raw))
         w4_sc.append(deal_scales("w4_sc1", w4_plane, 1))
-        tab_plane = zeroed_plane("tab_plane", T, tag="w4_raw")
-        load_scale_rows(nc.gpsimd, tab_plane, tab_scales)
-        wd_plane = zeroed_plane("wd_plane", H, tag="w4_plane")
-        load_scale_rows(nc.gpsimd, wd_plane, wd_scales)
         h2 = {}
         g2 = []
         wg2_turned = turn("wg2_turned", wg2_rows)
@@ -379,7 +379,7 @@ def tile_list_fog_net_yield_kernel(
             nc.sync.dma_start(dst[:], expect[2 * P * u : 2 * P * (u + 1), :].rearrange("(a p) j -> p a j", p=P))
             want.append(dst)
 
-        z_codes.append(new("zc1", [P, J], U32))
+        z_codes.append(new("zc1", [P, J], U32, tag="w4_raw"))
         z_scales.append(new("zs1", [P, J], U8, tag="w4_1"))
         for u in range(HALVES):
             quantize_z(1, u)

from contextlib import ExitStack

import concourse.mybir as mybir
from concourse.masks import make_identity

K, K2, H, N, T, S, T2, J = 1024, 512, 1024, 512, 2048, 512, 2048, 1024
FLOPS = 2 * (2 * K * H * S + K2 * H * S + H * N * J)

F32 = mybir.dt.float32
BF16 = mybir.dt.bfloat16
I32 = mybir.dt.int32
U32 = mybir.dt.uint32
U16 = mybir.dt.uint16
U8 = mybir.dt.uint8
FP8X4 = mybir.dt.float8_e4m3fn_x4
FP4X4 = mybir.dt.float4_e2m1fn_x4
ACT = mybir.ActivationFunctionType
ALU = mybir.AluOpType

P = 128
PACK = 4
KP = P * PACK
NB = 512
TILES = H // P
HALVES = J // NB
LAST = 64


def tile_list_fog_net_yield_kernel(
    tc, tab_words, tab_scales, tab2_words, tab2_scales, offs, offs2, offs3, offs4, offs5,
    w1, wd_words, wd_scales, w4_words, w4_scales, wg1, wg2, page0, go, w3, expect, out,
):
    nc = tc.nc
    with ExitStack() as ctx:
        sb = ctx.enter_context(tc.tile_pool(name="sb", bufs=1))
        ps = ctx.enter_context(tc.psum_pool(name="ps", bufs=4))

        def new(name, shape, dtype, tag=None, bufs=1):
            return sb.tile(shape, dtype, name=name, tag=tag or name, bufs=bufs, align_bytes=64)

        def load_list(name, src):
            dst = new(name, list(src.shape), U16)
            nc.sync.dma_start(dst[:], src)
            return dst

        def zeroed_plane(name, width, tag=None):
            plane = new(name, [P, width], U8, tag=tag)
            nc.gpsimd.memset(plane[:].bitcast(I32), 0)
            return plane

        def load_scale_rows(queue, plane, src):
            passes = src.shape[0]
            for q in range(4):
                queue.dma_start(
                    plane[32 * q : 32 * q + 4 * passes, :].bitcast(I32),
                    src[:, 4 * q : 4 * q + 4, :].bitcast(I32),
                )

        def load_words(name, src):
            dst = new(name, [P, T], I32)
            nc.sync.dma_start(dst[:], src.rearrange("p t i -> p (t i)").bitcast(I32))
            return dst

        def load_weights(name, src):
            dst = new(name, [P, S], F32, tag="h1", bufs=2)
            nc.sync.dma_start(dst[:], src)
            return dst

        def turn(name, src):
            bank = ps.tile([P, S], F32, name=name, tag="second")
            for c in range(S // P):
                nc.tensor.transpose(bank[:, P * c : P * (c + 1)], src[:, P * c : P * (c + 1)], ident[:])
            return bank

        def deal_weights(name, turned, t):
            spread = new(name + "s", [P, S], F32, tag="pd_sb", bufs=3)
            nc.scalar.copy(
                spread[:].rearrange("p (c q m) -> p c q m", q=4, m=32),
                turned[:].rearrange("p (c m t) -> p c t m", m=32, t=PACK)[:, :, t : t + 1, :].to_broadcast([P, S // P, 4, 32]),
            )
            dst = new(name, [P, S], F32)
            nc.scalar.copy(dst[:], turn(name + "t", spread)[:])
            return dst

        def load_page(i):
            b, t = divmod(i, PACK)
            dst = new("page%d" % i, [P, T2], F32)
            nc.sync.dma_start(dst[:], page0[KP * b : KP * (b + 1), :].rearrange("(p t) c -> p t c", t=PACK)[:, t, :])
            return dst

        def load_rows(name, src):
            dst = new(name, [P, PACK, NB], F32, tag="stage", bufs=3)
            nc.sync.dma_start(dst[:], src.rearrange("(p i) c -> p i c", i=PACK))
            return dst

        def load_w1(b, a):
            return load_rows("w1raw%d%d" % (b, a), w1[KP * a : KP * (a + 1), KP * b : KP * (b + 1)])

        def load_wd(b):
            dst = new("wdraw%d" % b, [P, 2, KP], I32, tag="ring4k", bufs=3)
            src = wd_words.rearrange("a p c i -> p a (c i)")[:, :, PACK * KP * b : PACK * KP * (b + 1)]
            nc.sync.dma_start(dst[:], src.bitcast(I32))
            return dst

        def gather_words(name, table, lst):
            dst = new(name, [P, S], U32)
            nc.vector.tensor_copy(dst[:], table[:].bitcast(U32).indirect(lst[:]))
            return dst

        def gather_scales(name, plane, lst):
            dst = new(name, [P, S], U8)
            nc.vector.tensor_copy(dst[:], plane[:].indirect(lst[:]))
            return dst

        def deal_scales(name, plane, b, tag=None):
            dst = new(name, [P, KP], U8, tag=tag)
            nc.vector.tensor_copy(
                dst[:].rearrange("p (t c e) -> p c t e", t=PACK, e=16),
                plane[:, KP * b : KP * (b + 1)].rearrange("p (c e t) -> p c t e", t=PACK, e=16),
            )
            return dst

        def deal_w4(b, raw):
            dst = new("w4_%d" % b, [P, 2 * KP], U8)
            nc.vector.tensor_copy(
                dst[:].bitcast(U16).rearrange("p (t c e) -> p c t e", t=PACK, e=8),
                raw[:, 2 * KP * b : 2 * KP * (b + 1)].bitcast(U16).rearrange("p (c e t) -> p c t e", t=PACK, e=8),
            )
            return dst

        def deal_wd(b, raw):
            dst = new("wd%d" % b, [P, 2 * KP], I32)
            nc.vector.tensor_copy(
                dst[:].rearrange("p (a t c e) -> p a c t e", a=2, t=PACK, e=4),
                raw[:].rearrange("p a (c e t) -> p a c t e", t=PACK, e=4),
            )
            return dst

        def quantize(name, grouped):
            codes = new(name + "c", [P, NB], U32)
            scales = new(name + "s", [P, NB], U8)
            nc.vector.quantize_mx(out=codes[:].bitcast(FP8X4), scales=scales[:], in_=grouped[:])
            return codes, scales

        def round_w1(name, raw):
            grouped = new(name, [P, PACK * NB], BF16, tag="ring4k", bufs=3)
            nc.scalar.copy(
                grouped[:].rearrange("p (t m i) -> p m i t", t=PACK, i=PACK),
                raw[:].rearrange("p i (m t) -> p m i t", t=PACK),
            )
            return grouped

        def round_w3(name, raw):
            grouped = new(name, [P, PACK * NB], BF16, tag="ring4k", bufs=3)
            nc.scalar.copy(
                grouped[:].rearrange("p (c e i) -> p c i e", e=PACK, i=PACK),
                raw[:].rearrange("p i (c e) -> p c i e", e=PACK),
            )
            return grouped

        tab2_plane = zeroed_plane("tab2_plane", T)
        w4_plane = zeroed_plane("w4_plane", H)
        ident = new("ident", [P, P], F32)
        make_identity(nc, ident[:])
        tab_plane = zeroed_plane("tab_plane", T)
        wd_plane = zeroed_plane("wd_plane", H)
        one = new("one", [P, 8], F32)
        nc.vector.memset(one[:], 1.0)
        warm = new("warm", [P, 8], F32)
        nc.scalar.activation(warm[:], one[:], ACT.Ln)

        idx2 = load_list("idx2", offs2)
        wg2_rows = load_weights("wg2_rows", wg2)
        w4_raw = new("w4_raw", [P, 2 * H], U8)
        nc.sync.dma_start(w4_raw[:].bitcast(I32), w4_words[0].bitcast(I32))
        load_scale_rows(nc.sync, tab2_plane, tab2_scales)
        tab2 = load_words("tab2", tab2_words[0])
        load_scale_rows(nc.sync, w4_plane, w4_scales)
        order = [PACK * b + t for t in range(PACK) for b in range(2)]
        pages = {order[0]: load_page(order[0])}
        idx4 = load_list("idx4", offs4)
        for step in (1, 2, 3):
            pages[order[step]] = load_page(order[step])
        load_scale_rows(nc.sync, tab_plane, tab_scales)
        w1_raw = {(0, 0): load_w1(0, 0)}
        pages[order[4]] = load_page(order[4])
        load_scale_rows(nc.sync, wd_plane, wd_scales)
        wg1_rows = load_weights("wg1_rows", wg1)
        pages[order[5]] = load_page(order[5])
        w1_raw[(0, 1)] = load_w1(0, 1)
        pages[order[6]] = load_page(order[6])
        idx = load_list("idx", offs)
        tab = [load_words("tab%d" % a, tab_words[a]) for a in range(2)]
        idx3 = load_list("idx3", offs3)
        wd_raw = [load_wd(0)]
        pages[order[7]] = load_page(order[7])
        idx5 = load_list("idx5", offs5)
        gain = new("gain", [P, 2, PACK], F32)
        nc.sync.dma_start(gain[:], go.rearrange("(b p t) -> p b t", b=2, t=PACK))

        w4 = [deal_w4(0, w4_raw)]
        v2_scales = gather_scales("v2_scales", tab2_plane, idx2)
        v2 = gather_words("v2", tab2, idx2)
        w4_sc = [deal_scales("w4_sc0", w4_plane, 0)]
        w4.append(deal_w4(1, w4_raw))
        w4_sc.append(deal_scales("w4_sc1", w4_plane, 1))
        h2 = {}
        g2 = []
        wg2_turned = turn("wg2_turned", wg2_rows)
        for i in order:
            b, t = divmod(i, PACK)
            if b == 0:
                g2.append(deal_weights("g2_%d" % t, wg2_turned, t))
            bank = ps.tile([P, S], F32, name="t2_%d" % i, tag="first")
            nc.tensor.matmul_mx(
                out=bank[:],
                lhsT=w4[b][:, 2 * P * t : 2 * P * (t + 1)].bitcast(FP4X4),
                lhsT_scale=w4_sc[b][:, P * t : P * (t + 1)],
                rhs=v2[:].bitcast(FP8X4),
                rhs_scale=v2_scales[:],
                start=True,
                stop=True,
            )
            if i == TILES - 1:
                h = new("h2_%d" % i, [P, S], F32, tag="hold_a")
            else:
                h = new("h2_%d" % i, [P, S], F32, tag="h2", bufs=TILES - 1)
            for lo in (0, S // 2):
                nc.scalar.activation(h[:, lo : lo + S // 2], bank[:, lo : lo + S // 2], ACT.Abs)
            for lo in (0, S // 2):
                nc.scalar.activation(h[:, lo : lo + S // 2], h[:, lo : lo + S // 2], ACT.Ln, bias=1.0)
            h2[i] = h

        def put(i, lst, h, weights):
            nc.vector.tensor_tensor(pages[i][:].indirect(lst[:]), h[:], weights[i % PACK][:], ALU.mult)

        w1q = {}
        for step in range(TILES - 1):
            i = order[step]
            put(i, idx4, h2[i], g2)
            if step in (4, 6):
                a = (step - 4) // 2
                w1q[(0, a)] = quantize("w1q0%d" % a, round_w1("w1b0%d" % a, w1_raw[(0, a)]))
        wg1_turned = turn("wg1_turned", wg1_rows)
        g1 = [deal_weights("g1_%d" % t, wg1_turned, t) for t in range(PACK)]
        v = [gather_words("v%d" % a, tab[a], idx) for a in range(2)]
        v_scales = gather_scales("v_scales", tab_plane, idx)
        wd_sc = [deal_scales("wd_sc0", wd_plane, 0, tag="g2_2")]
        wd = [deal_wd(0, wd_raw[0])]
        put(TILES - 1, idx4, h2[TILES - 1], g2)

        w1_raw[(1, 0)] = load_w1(1, 0)
        w1_raw[(1, 1)] = load_w1(1, 1)
        wd_raw.append(load_wd(1))

        def droplet_sums(i):
            b, t = divmod(i, PACK)
            cols = slice(P * t, P * (t + 1))
            p1 = ps.tile([P, S], F32, name="p1_%d" % i, tag="first")
            for a in range(2):
                codes, scales = w1q[(b, a)]
                nc.tensor.matmul_mx(
                    out=p1[:], lhsT=codes[:, cols].bitcast(FP8X4), lhsT_scale=scales[:, cols],
                    rhs=v[a][:].bitcast(FP8X4), rhs_scale=v_scales[4 * a : P, :],
                    start=(a == 0), stop=(a == 1),
                )
            pd = ps.tile([P, S], F32, name="pd_%d" % i, tag="first")
            for a in range(2):
                nc.tensor.matmul_mx(
                    out=pd[:],
                    lhsT=wd[b][:, KP * a + P * t : KP * a + P * (t + 1)].bitcast(FP8X4),
                    lhsT_scale=wd_sc[b][4 * a : P, cols],
                    rhs=v[a][:].bitcast(FP8X4), rhs_scale=v_scales[4 * a : P, :],
                    start=(a == 0), stop=(a == 1),
                )
            pd_sb = new("pd_sb%d" % i, [P, S], F32, tag="pd_sb", bufs=3)
            nc.scalar.copy(pd_sb[:], pd[:])
            return p1, pd_sb

        def maximum(i, sums):
            if i == 0:
                h = new("h1_%d" % i, [P, S], F32, tag="hold_a")
            elif i == 5:
                h = new("h1_%d" % i, [P, S], F32, tag="hold_b")
            else:
                h = new("h1_%d" % i, [P, S], F32, tag="h1", bufs=2)
            nc.vector.tensor_tensor(h[:], sums[0][:], sums[1][:], ALU.max)
            return h

        sums = {i: droplet_sums(i) for i in range(2)}
        for a in range(2):
            w1q[(1, a)] = quantize("w1q1%d" % a, round_w1("w1b1%d" % a, w1_raw[(1, a)]))
        wd.append(deal_wd(1, wd_raw[1]))
        wd_sc.append(deal_scales("wd_sc1", wd_plane, 1, tag="g2_3"))
        w3_raw = [load_rows("w3raw%d" % b, w3[KP * b : KP * (b + 1), :]) for b in range(2)]
        h1 = {0: maximum(0, sums[0])}
        sums[2] = droplet_sums(2)

        z_codes, z_scales, w3q = [], [], []
        z_rows = {}
        z = {}

        def weave(engine_copy, u, first, count):
            engine_copy(
                z[u][:].rearrange("p (c e t) -> p c t e", e=PACK, t=PACK)[:, :, first : first + count, :],
                z_rows[u][:, first : first + count, :].rearrange("p t (c e) -> p c t e", e=PACK),
            )

        def quantize_z(b, u):
            cols = slice(NB * u, NB * (u + 1))
            nc.vector.quantize_mx(out=z_codes[b][:, cols].bitcast(FP8X4), scales=z_scales[b][:, cols], in_=z[u][:])

        scores = {}

        def yield_pass(u, n, b):
            cols = slice(NB * u, NB * (u + 1))
            rows = slice(P * n, P * (n + 1))
            if b == 0:
                scores[(u, n)] = ps.tile([P, NB], F32, name="y%d%d" % (u, n), tag="second" if u == 0 else "first")
            codes, scales = w3q[b]
            nc.tensor.matmul_mx(
                out=scores[(u, n)][:], lhsT=codes[:, rows].bitcast(FP8X4), lhsT_scale=scales[:, rows],
                rhs=z_codes[b][:, cols].bitcast(FP8X4), rhs_scale=z_scales[b][:, cols],
                start=(b == 0), stop=(b == 1),
            )

        for i in range(TILES):
            b, t = divmod(i, PACK)
            put(i, idx3, h1[i], g1)
            if i + 1 < TILES:
                h1[i + 1] = maximum(i + 1, sums[i + 1])
            if i == 5:
                z_codes.append(new("zc0", [P, J], U32, tag="hold_b"))
                z_scales.append(new("zs0", [P, J], U8, tag="w4_0"))
                for u in range(HALVES):
                    quantize_z(0, u)
            if i >= TILES - 2:
                for n in range(N // P):
                    yield_pass(i - (TILES - 2), n, 0)
            if t == 0:
                z_rows[0] = new("z_rows%d0" % b, [P, PACK, NB], BF16, tag="g2_0")
                z_rows[1] = new("z_rows%d1" % b, [P, PACK, NB], BF16, tag="g2_1")
            picked = new("picked%d" % i, [P, J], F32, tag="picked", bufs=2)
            pieces = HALVES if i == TILES - 1 else 1
            width = J // pieces
            for u in range(pieces):
                cols = slice(width * u, width * (u + 1))
                lst = idx5[:, width // 16 * u : width // 16 * (u + 1)]
                nc.vector.tensor_copy(picked[:, cols], pages[i][:].indirect(lst))
            factor = gain[:, b, t : t + 1]
            if i == TILES - 1:
                for u in range(HALVES):
                    cols = slice(NB * u, NB * (u + 1))
                    nc.scalar.activation(picked[:, cols], picked[:, cols], ACT.Tanh)
                    nc.scalar.activation(z_rows[u][:, t, :], picked[:, cols], ACT.Copy, scale=factor)
                for u in range(HALVES):
                    weave(nc.vector.tensor_copy, u, 2, 2)
            else:
                for u in range(HALVES):
                    cols = slice(NB * u, NB * (u + 1))
                    nc.scalar.activation(picked[:, cols], picked[:, cols], ACT.Tanh)
                for lo, hi in ((0, NB), (NB, J - LAST), (J - LAST, J)):
                    if hi == J and i + 3 < TILES:
                        sums[i + 3] = droplet_sums(i + 3)
                    u = lo // NB
                    nc.scalar.activation(
                        z_rows[u][:, t, lo - NB * u : hi - NB * u], picked[:, lo:hi], ACT.Copy, scale=factor
                    )
            if i in (3, 5):
                for u in range(HALVES):
                    z[u] = new("z%d%d" % (b, u), [P, PACK * NB], BF16, tag="z%d" % u)
                    weave(nc.scalar.copy, u, 0, PACK if b == 0 else 2)
            if i in (0, 1):
                w3q.append(quantize("w3q%d" % i, round_w3("w3b%d" % i, w3_raw[i])))

        want = []
        for u in range(2):
            dst = new("want%d" % u, [P, 2, J], F32, tag="stage", bufs=3)
            nc.sync.dma_start(dst[:], expect[2 * P * u : 2 * P * (u + 1), :].rearrange("(a p) j -> p a j", p=P))
            want.append(dst)

        z_codes.append(new("zc1", [P, J], U32, tag="w4_raw"))
        z_scales.append(new("zs1", [P, J], U8, tag="w4_1"))
        for u in range(HALVES):
            quantize_z(1, u)
        for u in range(HALVES):
            cols = slice(NB * u, NB * (u + 1))
            for n in range(N // P):
                rows = slice(P * n, P * (n + 1))
                yield_pass(u, n, 1)
                y = scores[(u, n)]
                diff = new("diff%d%d" % (u, n), [P, NB], F32, tag="h2", bufs=TILES - 1)
                nc.vector.tensor_tensor(diff[:], y[:], want[n // 2][:, n % 2, cols], ALU.subtract)
                nc.scalar.activation(diff[:], diff[:], ACT.Square)
                nc.sync.dma_start(out[rows, cols], diff[:])
